import numpy as np
import ml_dtypes


def mxq(x, axis, fmt="e4m3"):
    dtype, down = {"e4m3": (ml_dtypes.float8_e4m3fn, 7), "e5m2": (ml_dtypes.float8_e5m2, 14)}[fmt]
    v = np.moveaxis(np.asarray(x, np.float32).astype(ml_dtypes.bfloat16).astype(np.float64), axis, -1)
    blocks = v.reshape(v.shape[:-1] + (-1, 32))
    amax = np.abs(blocks).max(-1, keepdims=True)
    byte = np.maximum(np.where(amax > 0, np.frexp(amax)[1] - 1 + 127, 0) - down, 1)
    scale = np.exp2(byte - 127.0)
    codes = (blocks / scale).astype(np.float32).astype(dtype).astype(np.float64)
    return np.moveaxis((codes * scale).reshape(v.shape), -1, axis)


WIDE = False


def mx_kscale(k):
    if not WIDE:
        return np.ones(k)
    levels = np.array([10, -10, 5, -5, 0])
    if k % 512:
        return np.exp2(np.random.permutation(np.resize(levels, k // 32))).repeat(32)
    a = np.empty((k // 512, 16))
    for p in range(k // 512):
        a[p, :8] = np.random.permutation(np.resize(levels, 8))
        for g in range(8):
            far = levels[np.abs(levels - a[p, g]) >= 10]
            a[p, g + 8] = far[np.random.randint(len(far))]
    return np.exp2(a.ravel()).repeat(32)


def f64(x):
    return np.asarray(x).astype(np.float64)


def striped(idx):
    return np.tile(idx.reshape(-1, 16).T, (8, 1)).astype(np.uint16)


def unstriped(offs):
    return offs[:16].T.reshape(-1).astype(np.int64)


def pack_weight(w):
    k, n = w.shape
    w = f64(np.asarray(w, np.float32).astype(ml_dtypes.bfloat16)).reshape(k // 32, 32, n)
    amax = np.abs(w).max(1)
    byte = np.clip(np.where(amax > 0, np.frexp(amax)[1] - 1 + 127 - 7, 1), 1, 254)
    scaled = (w * np.exp2(127.0 - byte)[:, None, :]).reshape(k, n).astype(np.float32)
    words = np.ascontiguousarray(scaled.reshape(k // 512, 128, 4, n).transpose(0, 1, 3, 2)).astype(ml_dtypes.float8_e4m3fn).view(np.uint8)
    return words, np.ascontiguousarray(byte.astype(np.uint8).reshape(k // 512, 16, n))


def unpack_weight(words, scales):
    g, p, n, _ = words.shape
    vals = np.ascontiguousarray(words).view(ml_dtypes.float8_e4m3fn).astype(np.float64) * np.repeat(np.exp2(scales.astype(np.float64) - 127.0), 8, axis=1)[..., None]
    return vals.transpose(0, 1, 3, 2).reshape(g * 512, n)


E2M1 = np.array([0.0, 0.5, 1.0, 1.5, 2.0, 3.0, 4.0, 6.0, -0.0, -0.5, -1.0, -1.5, -2.0, -3.0, -4.0, -6.0])


def pack_fp4(w):
    k, n = w.shape
    w = f64(np.asarray(w, np.float32).astype(ml_dtypes.bfloat16)).reshape(k // 32, 32, n)
    amax = np.abs(w).max(1)
    mant, ex = np.frexp(amax / 6.0)
    byte = np.clip(np.where(amax > 0, np.where(mant > 0.5, ex, ex - 1) + 127, 1), 1, 254)
    scaled = (w * np.exp2(127.0 - byte)[:, None, :]).reshape(k, n).astype(np.float32)
    c = np.ascontiguousarray(scaled.reshape(k // 512, 128, 4, n).transpose(0, 1, 3, 2)).astype(ml_dtypes.float4_e2m1fn).view(np.uint8) & 0xF
    words = (c[..., 0::2] | (c[..., 1::2] << 4)).reshape(k // 512, 128, 2 * n)
    return np.ascontiguousarray(words), np.ascontiguousarray(byte.astype(np.uint8).reshape(k // 512, 16, n))


def unpack_fp4(words, scales):
    g, _, n = scales.shape
    words = np.ascontiguousarray(words).reshape(g, 128, n, 2)
    nib = np.empty((g, 128, n, 4), np.uint8)
    nib[..., 0::2] = words & 0xF
    nib[..., 1::2] = words >> 4
    vals = E2M1[nib] * np.repeat(np.exp2(scales.astype(np.float64) - 127.0), 8, axis=1)[..., None]
    return vals.transpose(0, 1, 3, 2).reshape(g * 512, n)


K, T, S, N, H = 1024, 1024, 512, 128, 512


def setup_inputs():
    n = np.random.standard_normal
    s = mx_kscale(K)[:, None]
    u = mx_kscale(H)
    packed_xT = pack_weight(n((K, T)) * s)
    packed_w1 = pack_fp4(n((K, H)) / np.sqrt(K) / s)
    packed_w2 = pack_fp4(n((K, H)) / np.sqrt(K) / s)
    packed_w3 = pack_fp4(n((H, N)) / np.sqrt(H) / u[:, None])
    return {
        "x_words": packed_xT[0],
        "x_scales": packed_xT[1],
        "w1_words": packed_w1[0],
        "w1_scales": packed_w1[1],
        "w2_words": packed_w2[0],
        "w2_scales": packed_w2[1],
        "rest": (0.5 * n((H, S))).astype(np.float32),
        "stf": (np.random.uniform(0.5, 1.5, (H, 1))).astype(np.float32),
        "unit": (np.random.uniform(0.6, 1.4, (H, 1)) * u[:, None]).astype(np.float32),
        "w3_words": packed_w3[0],
        "w3_scales": packed_w3[1],
        "offs": striped(np.random.permutation(T)[:S]),
        "nx": striped(np.random.permutation(S)),
    }


def reference(x_words, x_scales, w1_words, w1_scales, w2_words, w2_scales, rest, stf, unit, w3_words, w3_scales, offs, nx):
    xq = unpack_weight(x_words, x_scales)[:, unstriped(offs)]
    et = unpack_fp4(w2_words, w2_scales).T @ xq
    tn = et[:, unstriped(nx)]
    twist = tn - et
    ex = unpack_fp4(w1_words, w1_scales).T @ xq
    e0 = 0.5 * np.tanh(ex) + 1.0
    e1 = e0[:, unstriped(nx)]
    bin_ = ((2.0 * np.tanh(twist)) * e1) / (e0 * e1 + (0.5 * e0) ** 2 + 0.3)
    bend = (bin_ - f64(rest)) ** 2
    ener = f64(stf) * bend + 0.3 * ((twist) ** 2)
    mom = bin_ * ener
    hid = f64(unit) * (mom - bin_[:, unstriped(nx)])
    return unpack_fp4(w3_words, w3_scales).T @ mxq(hid, 0, "e4m3")

@@ -1,0 +1,271 @@
+import math
+from contextlib import ExitStack
+
+import concourse.mybir as mybir
+
+K, T, S, N, H = 1024, 1024, 512, 128, 512
+FLOPS = 2 * S * (2 * K * H + H * N)
+
+F32 = mybir.dt.float32
+BF16 = mybir.dt.bfloat16
+I32 = mybir.dt.int32
+U32 = mybir.dt.uint32
+U16 = mybir.dt.uint16
+U8 = mybir.dt.uint8
+FP8X4 = mybir.dt.float8_e4m3fn_x4
+FP4X4 = mybir.dt.float4_e2m1fn_x4
+ALU = mybir.AluOpType
+ACT = mybir.ActivationFunctionType
+
+P = 128
+PACK = 4
+PASSES = K // (P * PACK)
+QUADS = 4
+HALF = S // 2
+OUT_CHUNKS = [(0, 256), (256, 384), (384, 512)]
+
+
+def tile_picked_ybinor_mom_p_kernel(
+    tc, x_words, x_scales, w1_words, w1_scales, w2_words, w2_scales, rest, stf, unit, w3_words, w3_scales, offs, nx, out
+):
+    nc = tc.nc
+    with ExitStack() as ctx:
+        lists = ctx.enter_context(tc.tile_pool(name="lists", bufs=1))
+        keep = ctx.enter_context(tc.tile_pool(name="keep", bufs=1))
+        psum = ctx.enter_context(tc.psum_pool(name="psum", bufs=8))
+
+        offs_sb = lists.tile([P, S // 16], U16, name="offs_sb")
+        nx_sb = lists.tile([P, S // 16], U16, name="nx_sb")
+
+        xw = [keep.tile([P, T], I32, name=f"xw{o}", align_bytes=64) for o in range(PASSES)]
+        xs = keep.tile([P, PASSES * T], U8, name="xs", align_bytes=64)
+        ww_raw = [keep.tile([P, PASSES * 2 * H], U8, name=f"ww_raw{w}", align_bytes=64) for w in range(2)]
+        ws_raw = [keep.tile([P, PASSES * H], U8, name=f"ws_raw{w}", align_bytes=64) for w in range(2)]
+        stf_sb = keep.tile([P, PACK], F32, name="stf_sb")
+        unit_sb = keep.tile([P, PACK], F32, name="unit_sb")
+        win = [keep.tile([P, 4 * S], F32, name=f"win{a}") for a in range(PACK)]
+
+        nc.vector.memset(xs[:].bitcast(I32), 0)
+        for w in range(2):
+            nc.gpsimd.memset(ws_raw[w][:].bitcast(I32), 0)
+        for a in range(PACK):
+            (nc.vector if a < 2 else nc.gpsimd).memset(win[a][:, 2 * S : 4 * S], 0.0)
+
+        def load_scales(queue, dst, src, passes):
+            for q in range(QUADS):
+                queue.dma_start(
+                    out=dst[32 * q : 32 * q + 4, :].bitcast(I32).rearrange("r (o c) -> r o c", o=passes),
+                    in_=src[:, 4 * q : 4 * q + 4, :].bitcast(I32).rearrange("o r c -> r o c"),
+                )
+
+        def load_words(dst, src):
+            nc.sync.dma_start(
+                out=dst.bitcast(I32).rearrange("p (o c) -> p o c", o=PASSES),
+                in_=src.bitcast(I32).rearrange("o p c -> p o c"),
+            )
+
+        nc.sync.dma_start(offs_sb[:], offs)
+        for o in range(PASSES):
+            nc.sync.dma_start(out=xw[o][:], in_=x_words[o].rearrange("p c r -> p (c r)").bitcast(I32))
+        load_scales(nc.sync, xs, x_scales, PASSES)
+        load_words(ww_raw[0][:], w2_words)
+        load_scales(nc.sync, ws_raw[0], w2_scales, PASSES)
+        load_words(ww_raw[1][:], w1_words)
+        load_scales(nc.sync, ws_raw[1], w1_scales, PASSES)
+        nc.sync.dma_start(nx_sb[:], nx)
+        nc.gpsimd.dma_start(out=unit_sb[:], in_=unit.rearrange("(p a) o -> p (a o)", a=PACK))
+        nc.gpsimd.dma_start(out=stf_sb[:], in_=stf.rearrange("(p a) o -> p (a o)", a=PACK))
+
+        gs = [keep.tile([P, S], U8, name=f"gs{o}", align_bytes=64) for o in range(PASSES)]
+        gw = [keep.tile([P, S], U32, name=f"gw{o}", align_bytes=64) for o in range(PASSES)]
+
+        groups = PASSES * P
+        later = PACK - 1
+        ww_first = [keep.tile([P, 2 * groups], U8, name=f"ww_first{w}", align_bytes=64) for w in range(2)]
+        ws_first = [keep.tile([P, groups], U8, name=f"ws_first{w}", align_bytes=64) for w in range(2)]
+        ww_cols = [ww_raw[w][:].bitcast(U16).rearrange("p (g a) -> p g a", a=PACK) for w in range(2)]
+        ws_cols = [ws_raw[w][:].rearrange("p (g a) -> p g a", a=PACK) for w in range(2)]
+        ww = [[ww_first[w][:]] for w in range(2)]
+        ws = [[ws_first[w][:]] for w in range(2)]
+
+        def one_pass(acc, a, w, o):
+            nc.tensor.matmul_mx(
+                out=acc[:],
+                lhsT=ww[w][a][:, 2 * o * P : 2 * (o + 1) * P].bitcast(FP4X4),
+                lhsT_scale=ws[w][a][:, o * P : (o + 1) * P],
+                rhs=gw[o][:].bitcast(FP8X4),
+                rhs_scale=gs[o][:],
+                start=(o == 0),
+                stop=(o == PASSES - 1),
+            )
+
+        def plane(name, count=PACK):
+            return [keep.tile([P, S], F32, name=f"{name}{a}")[:] for a in range(count)]
+
+        th = [win[a][:, 0:S] for a in range(PACK)]
+        et = [win[a][:, S : 2 * S] for a in range(PACK)]
+        roots = keep.tile([P, 2 * S], F32, name="roots")
+        v_late = keep.tile([P, 2 * S], F32, name="v_late")
+        binu_nx = [keep.tile([P, PACK * HALF], F32, name=f"binu_nx{h}") for h in range(2)]
+        tw = plane("tw", PACK - 1) + [roots[:, HALF : HALF + S]]
+        tn = plane("tn", PACK - 1) + [v_late[:, HALF : HALF + S]]
+        v = plane("v", 2) + [v_late[:, 0:S], v_late[:, S : 2 * S]]
+        d = [binu_nx[a // 2][:, (a % 2) * S : (a % 2 + 1) * S] for a in range(PACK)]
+        root = [roots[:, (a % 2) * S : (a % 2 + 1) * S] for a in range(PACK)]
+        turn, tw2, y1, y, num, rec, binu, bend, ener = (
+            plane(nm) for nm in ("turn", "tw2", "y1", "y", "num", "rec", "binu", "bend", "ener")
+        )
+        momu = keep.tile([P, PACK, S], F32, name="momu")
+
+        first = [psum.tile([P, S], F32, name="acc") for w in range(2)]
+        for o in range(PASSES):
+            nc.vector.tensor_copy(gw[o][:], xw[o][:].bitcast(U32).indirect(offs_sb[:]))
+            if o == 1:
+                nc.vector.tensor_copy(ww_first[1][:].bitcast(U16), ww_cols[1][:, :, 0])
+                nc.vector.tensor_copy(ws_first[1][:], ws_cols[1][:, :, 0])
+                one_pass(first[1], 0, 1, 0)
+            nc.vector.tensor_copy(gs[o][:], xs[:, o * T : (o + 1) * T].indirect(offs_sb[:]))
+            if o == 0:
+                nc.vector.tensor_copy(ww_first[0][:].bitcast(U16), ww_cols[0][:, :, 0])
+                nc.vector.tensor_copy(ws_first[0][:], ws_cols[0][:, :, 0])
+                one_pass(first[0], 0, 0, 0)
+        for w in range(2):
+            one_pass(first[w], 0, w, 1)
+        dealt = keep.tile([P, 2, 3 * later * groups], U8, name="dealt", tag="xs", align_bytes=64)
+        ww_later = [dealt[:, w, 0 : 2 * later * groups].rearrange("p (a g) -> p a g", a=later) for w in range(2)]
+        ws_later = [dealt[:, w, 2 * later * groups :].rearrange("p (a g) -> p a g", a=later) for w in range(2)]
+        for w in range(2):
+            ww[w].extend(ww_later[w][:, a, :] for a in range(later))
+            ws[w].extend(ws_later[w][:, a, :] for a in range(later))
+            nc.vector.tensor_copy(ww_later[w].bitcast(U16).rearrange("p a g -> p g a"), ww_cols[w][:, :, 1:PACK])
+            nc.vector.tensor_copy(ws_later[w].rearrange("p a g -> p g a"), ws_cols[w][:, :, 1:PACK])
+        w3w = keep.tile([P, 2 * N], U8, name="w3w", tag="ww_raw0", align_bytes=64)
+        nc.sync.dma_start(out=w3w[:].bitcast(I32), in_=w3_words[0].bitcast(I32))
+        w3s = keep.tile([P, N], U8, name="w3s", tag="ws_raw0", align_bytes=64)
+        nc.gpsimd.memset(w3s[:].bitcast(I32), 0)
+        load_scales(nc.sync, w3s, w3_scales, 1)
+
+        for a in range(PACK):
+            if a == 0:
+                et_ps, ex_ps = first
+            else:
+                et_ps = psum.tile([P, S], F32, name="acc")
+                ex_ps = psum.tile([P, S], F32, name="acc")
+                for w, acc in enumerate((et_ps, ex_ps)):
+                    for o in range(PASSES):
+                        one_pass(acc, a, w, o)
+            if a % 2 == 1:
+                nc.vector.tensor_copy(et[a], et_ps[:])
+            else:
+                nc.scalar.activation(et[a], et_ps[:], ACT.Copy)
+            nc.scalar.activation(th[a], ex_ps[:], ACT.Tanh)
+            nc.scalar.activation(tn[a], win[a][:, S : 3 * S].indirect(nx_sb[:]), ACT.Copy)
+            nc.vector.tensor_tensor(tw[a], tn[a], et[a], ALU.subtract)
+            nc.scalar.activation(turn[a], tw[a], ACT.Tanh)
+        last = PACK - 1
+        nc.vector.scalar_tensor_tensor(tw2[last], tw[last], 0.3, tw[last], ALU.mult, ALU.mult)
+
+        rest_rows = rest.rearrange("(p a) c -> p a c", a=PACK)
+        rest_sb = [keep.tile([P, 2, S], F32, name=f"rest{o}", tag=f"gw{o}", align_bytes=64) for o in range(2)]
+        for o in range(2):
+            nc.sync.dma_start(out=rest_sb[o][:], in_=rest_rows[:, 2 * o : 2 * o + 2, :])
+        rs = [rest_sb[a // 2][:, a % 2, :] for a in range(PACK)]
+
+        for a in range(PACK):
+            nc.vector.tensor_scalar(v[a], win[a][:].indirect(nx_sb[:]), 1.0, 2.5, ALU.mult, ALU.add)
+            nc.vector.scalar_tensor_tensor(y1[a], th[a], 0.25, v[a], ALU.mult, ALU.add)
+            nc.vector.scalar_tensor_tensor(y[a], th[a], 2.0, y1[a], ALU.add, ALU.mult)
+            if a < 2:
+                nc.vector.scalar_tensor_tensor(num[a], v[a], -0.5, turn[a], ALU.add, ALU.mult)
+        for a in range(2, PACK):
+            nc.vector.scalar_tensor_tensor(num[a], v[a], -0.5, turn[a], ALU.add, ALU.mult)
+
+        safe = keep.tile([P, PACK], F32, name="safe", tag="ws_raw1", align_bytes=64)
+        uinv = keep.tile([P, PACK], F32, name="uinv")
+        nc.vector.scalar_tensor_tensor(safe[:], unit_sb[:], 0.0, unit_sb[:], ALU.is_equal, ALU.add)
+        nc.vector.reciprocal(uinv[:], safe[:])
+
+        def col(t, a):
+            return t[:, a : a + 1]
+
+        def roots_of(pair):
+            for a in pair:
+                nc.scalar.activation(root[a], y[a], ACT.Abs_reciprocal_sqrt, bias=0.3, scale=0.25)
+
+        def squares_of(pair):
+            for a in pair:
+                nc.scalar.activation(rec[a], root[a], ACT.Square)
+
+        def binormals(pair):
+            for a in pair:
+                nc.vector.scalar_tensor_tensor(binu[a], num[a], col(unit_sb, a), rec[a], ALU.mult, ALU.mult)
+
+        def distances(pair):
+            for a in pair:
+                nc.vector.scalar_tensor_tensor(d[a], binu[a], col(uinv, a), rs[a], ALU.mult, ALU.subtract)
+
+        def bends(pair):
+            for a in pair:
+                nc.scalar.activation(bend[a], d[a], ACT.Square)
+            for a in pair:
+                if a != last:
+                    nc.scalar.activation(tw2[a], tw[a], ACT.Square, scale=math.sqrt(0.3))
+
+        def energies(pair):
+            for a in pair:
+                nc.vector.scalar_tensor_tensor(ener[a], bend[a], col(stf_sb, a), tw2[a], ALU.mult, ALU.add)
+
+        def moments(pair):
+            for a in pair:
+                nc.vector.tensor_tensor(momu[:, a, :], binu[a], ener[a], ALU.mult)
+
+        early, late = (0, 1), (2, 3)
+        roots_of(early)
+        squares_of(early)
+        binormals(early)
+        roots_of(late)
+        distances(early)
+        squares_of(late)
+        bends(early)
+        binormals(late)
+        energies(early)
+        distances(late)
+        bends(late)
+        moments(early)
+        energies(late)
+        moments(late)
+        for h in range(2):
+            for a in range(PACK):
+                nc.scalar.activation(
+                    binu_nx[h][:, a * HALF : (a + 1) * HALF],
+                    binu[a].indirect(nx_sb[:, h * HALF // 16 : (h + 1) * HALF // 16]),
+                    ACT.Copy,
+                )
+
+        for c0, c1 in OUT_CHUNKS:
+            w = c1 - c0
+            hid = keep.tile([P, w * PACK], BF16, name=f"hid{c0}", align_bytes=64)
+            codes = keep.tile([P, w], U32, name=f"codes{c0}", align_bytes=64)
+            scales = keep.tile([P, w], U8, name=f"scales{c0}", align_bytes=64)
+            res = keep.tile([P, w], F32, name=f"res{c0}")
+            nc.vector.tensor_tensor(
+                hid[:].rearrange("p (c i a) -> p c a i", i=4, a=PACK),
+                momu[:, :, c0:c1].rearrange("p a (c i) -> p c a i", i=4),
+                binu_nx[c0 // HALF][:].rearrange("p (a n) -> p a n", a=PACK)[:, :, c0 % HALF : c0 % HALF + w].rearrange(
+                    "p a (c i) -> p c a i", i=4
+                ),
+                ALU.subtract,
+            )
+            nc.vector.quantize_mx(out=codes[:].bitcast(FP8X4), scales=scales[:], in_=hid[:])
+            acc = psum.tile([P, S], F32, name="acc")
+            nc.tensor.matmul_mx(
+                out=acc[:, 0:w],
+                lhsT=w3w[:].bitcast(FP4X4),
+                lhsT_scale=w3s[:],
+                rhs=codes[:].bitcast(FP8X4),
+                rhs_scale=scales[:],
+                start=True,
+                stop=True,
+            )
+            nc.scalar.activation(res[:], acc[:, 0:w], ACT.Copy)
+            nc.sync.dma_start(out=out[:, c0:c1], in_=res[:])

@@ -23,6 +23,7 @@ PASSES = K // (P * PACK)
 QUADS = 4
 HALF = S // 2
 OUT_CHUNKS = [(0, 256), (256, 384), (384, 512)]
+DEALS = [(0, 1), (1, 2), (2, 4)]
 
 
 def tile_picked_ybinor_mom_p_kernel(
@@ -36,149 +37,142 @@ def tile_picked_ybinor_mom_p_kernel(
 
         offs_sb = lists.tile([P, S // 16], U16, name="offs_sb")
         nx_sb = lists.tile([P, S // 16], U16, name="nx_sb")
+        nx_half = [nx_sb[:, h * HALF // 16 : (h + 1) * HALF // 16] for h in range(2)]
 
         xw = [keep.tile([P, T], I32, name=f"xw{o}", align_bytes=64) for o in range(PASSES)]
-        xs = keep.tile([P, PASSES * T], U8, name="xs", align_bytes=64)
+        xs = keep.tile([P, T], U8, name="xs", align_bytes=64)
         ww_raw = [keep.tile([P, PASSES * 2 * H], U8, name=f"ww_raw{w}", align_bytes=64) for w in range(2)]
         ws_raw = [keep.tile([P, PASSES * H], U8, name=f"ws_raw{w}", align_bytes=64) for w in range(2)]
+        gs = [keep.tile([P, S], U8, name=f"gs{o}", align_bytes=64) for o in range(PASSES)]
         stf_sb = keep.tile([P, PACK], F32, name="stf_sb")
         unit_sb = keep.tile([P, PACK], F32, name="unit_sb")
-        win = [keep.tile([P, 4 * S], F32, name=f"win{a}") for a in range(PACK)]
 
-        nc.vector.memset(xs[:].bitcast(I32), 0)
-        for w in range(2):
-            nc.gpsimd.memset(ws_raw[w][:].bitcast(I32), 0)
-        for a in range(PACK):
-            (nc.vector if a < 2 else nc.gpsimd).memset(win[a][:, 2 * S : 4 * S], 0.0)
+        for plane_tile in (xs, ws_raw[0], ws_raw[1], gs[1]):
+            nc.vector.memset(plane_tile[:].bitcast(I32), 0)
 
-        def load_scales(queue, dst, src, passes):
+        def load_scales(dst, src, passes):
             for q in range(QUADS):
-                queue.dma_start(
+                nc.sync.dma_start(
                     out=dst[32 * q : 32 * q + 4, :].bitcast(I32).rearrange("r (o c) -> r o c", o=passes),
                     in_=src[:, 4 * q : 4 * q + 4, :].bitcast(I32).rearrange("o r c -> r o c"),
                 )
 
-        def load_words(dst, src):
-            nc.sync.dma_start(
-                out=dst.bitcast(I32).rearrange("p (o c) -> p o c", o=PASSES),
-                in_=src.bitcast(I32).rearrange("o p c -> p o c"),
-            )
-
         nc.sync.dma_start(offs_sb[:], offs)
         for o in range(PASSES):
             nc.sync.dma_start(out=xw[o][:], in_=x_words[o].rearrange("p c r -> p (c r)").bitcast(I32))
-        load_scales(nc.sync, xs, x_scales, PASSES)
-        load_words(ww_raw[0][:], w2_words)
-        load_scales(nc.sync, ws_raw[0], w2_scales, PASSES)
-        load_words(ww_raw[1][:], w1_words)
-        load_scales(nc.sync, ws_raw[1], w1_scales, PASSES)
+        for q in range(QUADS):
+            nc.sync.dma_start(
+                out=xs[32 * q : 32 * q + 4 * PASSES, :].bitcast(I32),
+                in_=x_scales[:, 4 * q : 4 * q + 4, :].bitcast(I32),
+            )
+        for w, (words, scales) in enumerate(((w2_words, w2_scales), (w1_words, w1_scales))):
+            nc.sync.dma_start(
+                out=ww_raw[w][:].bitcast(I32).rearrange("p (o c) -> p o c", o=PASSES),
+                in_=words.bitcast(I32).rearrange("o p c -> p o c"),
+            )
+            load_scales(ws_raw[w], scales, PASSES)
         nc.sync.dma_start(nx_sb[:], nx)
         nc.gpsimd.dma_start(out=unit_sb[:], in_=unit.rearrange("(p a) o -> p (a o)", a=PACK))
         nc.gpsimd.dma_start(out=stf_sb[:], in_=stf.rearrange("(p a) o -> p (a o)", a=PACK))
 
-        gs = [keep.tile([P, S], U8, name=f"gs{o}", align_bytes=64) for o in range(PASSES)]
-        gw = [keep.tile([P, S], U32, name=f"gw{o}", align_bytes=64) for o in range(PASSES)]
-
-        groups = PASSES * P
-        later = PACK - 1
-        ww_first = [keep.tile([P, 2 * groups], U8, name=f"ww_first{w}", align_bytes=64) for w in range(2)]
-        ws_first = [keep.tile([P, groups], U8, name=f"ws_first{w}", align_bytes=64) for w in range(2)]
-        ww_cols = [ww_raw[w][:].bitcast(U16).rearrange("p (g a) -> p g a", a=PACK) for w in range(2)]
-        ws_cols = [ws_raw[w][:].rearrange("p (g a) -> p g a", a=PACK) for w in range(2)]
-        ww = [[ww_first[w][:]] for w in range(2)]
-        ws = [[ws_first[w][:]] for w in range(2)]
-
-        def one_pass(acc, a, w, o):
-            nc.tensor.matmul_mx(
-                out=acc[:],
-                lhsT=ww[w][a][:, 2 * o * P : 2 * (o + 1) * P].bitcast(FP4X4),
-                lhsT_scale=ws[w][a][:, o * P : (o + 1) * P],
-                rhs=gw[o][:].bitcast(FP8X4),
-                rhs_scale=gs[o][:],
-                start=(o == 0),
-                stop=(o == PASSES - 1),
+        gw_tags = ("gw0", "xs")
+        gw = [keep.tile([P, S], U32, name=f"gw{o}", tag=gw_tags[o], align_bytes=64) for o in range(PASSES)]
+        nc.vector.tensor_copy(gw[0][:], xw[0][:].bitcast(U32).indirect(offs_sb[:]))
+        nc.vector.tensor_copy(gs[0][:], xs[:].indirect(offs_sb[:]))
+        for q in range(QUADS):
+            nc.scalar.dma_start(
+                out=gs[1][32 * q : 32 * q + 4, :].bitcast(I32), in_=gs[0][32 * q + 4 : 32 * q + 8, :].bitcast(I32)
             )
+        nc.vector.tensor_copy(gw[1][:], xw[1][:].bitcast(U32).indirect(offs_sb[:]))
 
-        def plane(name, count=PACK):
+        cols = PASSES * P
+        ww_first = [keep.tile([P, 1, 2 * cols], U8, name=f"ww_first{w}", align_bytes=64) for w in range(2)]
+        ws_first = [keep.tile([P, 1, cols], U8, name=f"ws_first{w}", align_bytes=64) for w in range(2)]
+        later = PACK - 1
+        dealt = keep.tile([P, 2, 3 * later * cols], U8, name="dealt", tag="xw1", align_bytes=64)
+        ww_later = [dealt[:, w, 0 : 2 * later * cols].rearrange("p (a g) -> p a g", a=later) for w in range(2)]
+        ws_later = [dealt[:, w, 2 * later * cols :].rearrange("p (a g) -> p a g", a=later) for w in range(2)]
+
+        def dealt_words(w, a0, a1):
+            return ww_first[w][:] if a0 == 0 else ww_later[w][:, a0 - 1 : a1 - 1, :]
+
+        def dealt_scales(w, a0, a1):
+            return ws_first[w][:] if a0 == 0 else ws_later[w][:, a0 - 1 : a1 - 1, :]
+
+        for a0, a1 in DEALS:
+            for w in range(2):
+                word_cols = ww_raw[w][:].bitcast(U16).rearrange("p (g a) -> p a g", a=PACK)
+                scale_cols = ws_raw[w][:].rearrange("p (g a) -> p a g", a=PACK)
+                nc.vector.tensor_copy(dealt_words(w, a0, a1).bitcast(U16), word_cols[:, a0:a1, :])
+                nc.vector.tensor_copy(dealt_scales(w, a0, a1), scale_cols[:, a0:a1, :])
+
+        def product(a, w):
+            acc = psum.tile([P, S], F32, name="acc")
+            for o in range(PASSES):
+                nc.tensor.matmul_mx(
+                    out=acc[:],
+                    lhsT=dealt_words(w, a, a + 1)[:, 0, 2 * o * P : 2 * (o + 1) * P].bitcast(FP4X4),
+                    lhsT_scale=dealt_scales(w, a, a + 1)[:, 0, o * P : (o + 1) * P],
+                    rhs=gw[o][:].bitcast(FP8X4),
+                    rhs_scale=gs[o][:],
+                    start=(o == 0),
+                    stop=(o == PASSES - 1),
+                )
+            return acc
+
+        def planes(name, count=PACK):
             return [keep.tile([P, S], F32, name=f"{name}{a}")[:] for a in range(count)]
 
-        th = [win[a][:, 0:S] for a in range(PACK)]
-        et = [win[a][:, S : 2 * S] for a in range(PACK)]
+        last = PACK - 1
+        th_et = [keep.tile([P, 2 * S], F32, name=f"th_et{a}") for a in range(PACK)]
+        th = [th_et[a][:, 0:S] for a in range(PACK)]
+        et = [th_et[a][:, S : 2 * S] for a in range(PACK)]
         roots = keep.tile([P, 2 * S], F32, name="roots")
-        v_late = keep.tile([P, 2 * S], F32, name="v_late")
-        binu_nx = [keep.tile([P, PACK * HALF], F32, name=f"binu_nx{h}") for h in range(2)]
-        tw = plane("tw", PACK - 1) + [roots[:, HALF : HALF + S]]
-        tn = plane("tn", PACK - 1) + [v_late[:, HALF : HALF + S]]
-        v = plane("v", 2) + [v_late[:, 0:S], v_late[:, S : 2 * S]]
-        d = [binu_nx[a // 2][:, (a % 2) * S : (a % 2 + 1) * S] for a in range(PACK)]
         root = [roots[:, (a % 2) * S : (a % 2 + 1) * S] for a in range(PACK)]
-        turn, tw2, y1, y, num, rec, binu, bend, ener = (
-            plane(nm) for nm in ("turn", "tw2", "y1", "y", "num", "rec", "binu", "bend", "ener")
+        tw = planes("tw", last) + [roots[:, HALF : HALF + S]]
+        binu_nx = [keep.tile([P, PACK * HALF], F32, name=f"binu_nx{h}") for h in range(2)]
+        dist = [binu_nx[a // 2][:, (a % 2) * S : (a % 2 + 1) * S] for a in range(PACK)]
+        tn, turn, tw2, v, y1, y, num, rec, binu, bend, ener = (
+            planes(nm) for nm in ("tn", "turn", "tw2", "v", "y1", "y", "num", "rec", "binu", "bend", "ener")
         )
         momu = keep.tile([P, PACK, S], F32, name="momu")
 
-        first = [psum.tile([P, S], F32, name="acc") for w in range(2)]
-        for o in range(PASSES):
-            nc.vector.tensor_copy(gw[o][:], xw[o][:].bitcast(U32).indirect(offs_sb[:]))
-            if o == 1:
-                nc.vector.tensor_copy(ww_first[1][:].bitcast(U16), ww_cols[1][:, :, 0])
-                nc.vector.tensor_copy(ws_first[1][:], ws_cols[1][:, :, 0])
-                one_pass(first[1], 0, 1, 0)
-            nc.vector.tensor_copy(gs[o][:], xs[:, o * T : (o + 1) * T].indirect(offs_sb[:]))
-            if o == 0:
-                nc.vector.tensor_copy(ww_first[0][:].bitcast(U16), ww_cols[0][:, :, 0])
-                nc.vector.tensor_copy(ws_first[0][:], ws_cols[0][:, :, 0])
-                one_pass(first[0], 0, 0, 0)
-        for w in range(2):
-            one_pass(first[w], 0, w, 1)
-        dealt = keep.tile([P, 2, 3 * later * groups], U8, name="dealt", tag="xs", align_bytes=64)
-        ww_later = [dealt[:, w, 0 : 2 * later * groups].rearrange("p (a g) -> p a g", a=later) for w in range(2)]
-        ws_later = [dealt[:, w, 2 * later * groups :].rearrange("p (a g) -> p a g", a=later) for w in range(2)]
-        for w in range(2):
-            ww[w].extend(ww_later[w][:, a, :] for a in range(later))
-            ws[w].extend(ws_later[w][:, a, :] for a in range(later))
-            nc.vector.tensor_copy(ww_later[w].bitcast(U16).rearrange("p a g -> p g a"), ww_cols[w][:, :, 1:PACK])
-            nc.vector.tensor_copy(ws_later[w].rearrange("p a g -> p g a"), ws_cols[w][:, :, 1:PACK])
-        w3w = keep.tile([P, 2 * N], U8, name="w3w", tag="ww_raw0", align_bytes=64)
-        nc.sync.dma_start(out=w3w[:].bitcast(I32), in_=w3_words[0].bitcast(I32))
-        w3s = keep.tile([P, N], U8, name="w3s", tag="ws_raw0", align_bytes=64)
-        nc.gpsimd.memset(w3s[:].bitcast(I32), 0)
-        load_scales(nc.sync, w3s, w3_scales, 1)
-
-        for a in range(PACK):
-            if a == 0:
-                et_ps, ex_ps = first
-            else:
-                et_ps = psum.tile([P, S], F32, name="acc")
-                ex_ps = psum.tile([P, S], F32, name="acc")
-                for w, acc in enumerate((et_ps, ex_ps)):
-                    for o in range(PASSES):
-                        one_pass(acc, a, w, o)
-            if a % 2 == 1:
+        def up_to_tanh(a):
+            et_ps = product(a, 0)
+            ex_ps = product(a, 1)
+            if a == last:
                 nc.vector.tensor_copy(et[a], et_ps[:])
             else:
                 nc.scalar.activation(et[a], et_ps[:], ACT.Copy)
             nc.scalar.activation(th[a], ex_ps[:], ACT.Tanh)
-            nc.scalar.activation(tn[a], win[a][:, S : 3 * S].indirect(nx_sb[:]), ACT.Copy)
+            for h in range(2):
+                nc.vector.tensor_copy(tn[a][:, h * HALF : (h + 1) * HALF], et[a].indirect(nx_half[h]))
             nc.vector.tensor_tensor(tw[a], tn[a], et[a], ALU.subtract)
             nc.scalar.activation(turn[a], tw[a], ACT.Tanh)
-        last = PACK - 1
-        nc.vector.scalar_tensor_tensor(tw2[last], tw[last], 0.3, tw[last], ALU.mult, ALU.mult)
 
-        rest_rows = rest.rearrange("(p a) c -> p a c", a=PACK)
-        rest_sb = [keep.tile([P, 2, S], F32, name=f"rest{o}", tag=f"gw{o}", align_bytes=64) for o in range(2)]
-        for o in range(2):
-            nc.sync.dma_start(out=rest_sb[o][:], in_=rest_rows[:, 2 * o : 2 * o + 2, :])
-        rs = [rest_sb[a // 2][:, a % 2, :] for a in range(PACK)]
-
-        for a in range(PACK):
-            nc.vector.tensor_scalar(v[a], win[a][:].indirect(nx_sb[:]), 1.0, 2.5, ALU.mult, ALU.add)
+        def fraction(a):
+            nc.scalar.activation(v[a], th_et[a][:].indirect(nx_sb[:]), ACT.Copy, bias=2.5)
             nc.vector.scalar_tensor_tensor(y1[a], th[a], 0.25, v[a], ALU.mult, ALU.add)
             nc.vector.scalar_tensor_tensor(y[a], th[a], 2.0, y1[a], ALU.add, ALU.mult)
-            if a < 2:
-                nc.vector.scalar_tensor_tensor(num[a], v[a], -0.5, turn[a], ALU.add, ALU.mult)
-        for a in range(2, PACK):
             nc.vector.scalar_tensor_tensor(num[a], v[a], -0.5, turn[a], ALU.add, ALU.mult)
+
+        up_to_tanh(0)
+        fraction(0)
+        for a in range(1, PACK):
+            up_to_tanh(a)
+        nc.vector.scalar_tensor_tensor(tw2[last], tw[last], 0.3, tw[last], ALU.mult, ALU.mult)
+        for a in range(1, PACK):
+            fraction(a)
+
+        rest_rows = rest.rearrange("(p a) c -> p a c", a=PACK)
+        rest_sb = [keep.tile([P, 2, S], F32, name=f"rest{o}", tag=gw_tags[o], align_bytes=64) for o in range(2)]
+        for o in range(2):
+            nc.sync.dma_start(out=rest_sb[o][:], in_=rest_rows[:, 2 * o : 2 * o + 2, :])
+        w3w = keep.tile([P, 2 * N], U8, name="w3w", tag="gs0", align_bytes=64)
+        nc.sync.dma_start(out=w3w[:].bitcast(I32), in_=w3_words[0].bitcast(I32))
+        w3s = keep.tile([P, N], U8, name="w3s", tag="gs1", align_bytes=64)
+        nc.gpsimd.memset(w3s[:].bitcast(I32), 0)
+        load_scales(w3s, w3_scales, 1)
 
         safe = keep.tile([P, PACK], F32, name="safe", tag="ws_raw1", align_bytes=64)
         uinv = keep.tile([P, PACK], F32, name="uinv")
@@ -188,11 +182,11 @@ def tile_picked_ybinor_mom_p_kernel(
         def col(t, a):
             return t[:, a : a + 1]
 
-        def roots_of(pair):
+        def inverse_roots(pair):
             for a in pair:
                 nc.scalar.activation(root[a], y[a], ACT.Abs_reciprocal_sqrt, bias=0.3, scale=0.25)
 
-        def squares_of(pair):
+        def reciprocals(pair):
             for a in pair:
                 nc.scalar.activation(rec[a], root[a], ACT.Square)
 
@@ -202,11 +196,13 @@ def tile_picked_ybinor_mom_p_kernel(
 
         def distances(pair):
             for a in pair:
-                nc.vector.scalar_tensor_tensor(d[a], binu[a], col(uinv, a), rs[a], ALU.mult, ALU.subtract)
+                nc.vector.scalar_tensor_tensor(
+                    dist[a], binu[a], col(uinv, a), rest_sb[a // 2][:, a % 2, :], ALU.mult, ALU.subtract
+                )
 
-        def bends(pair):
+        def squares(pair):
             for a in pair:
-                nc.scalar.activation(bend[a], d[a], ACT.Square)
+                nc.scalar.activation(bend[a], dist[a], ACT.Square)
             for a in pair:
                 if a != last:
                     nc.scalar.activation(tw2[a], tw[a], ACT.Square, scale=math.sqrt(0.3))
@@ -220,52 +216,47 @@ def tile_picked_ybinor_mom_p_kernel(
                 nc.vector.tensor_tensor(momu[:, a, :], binu[a], ener[a], ALU.mult)
 
         early, late = (0, 1), (2, 3)
-        roots_of(early)
-        squares_of(early)
+        inverse_roots(early)
+        reciprocals(early)
         binormals(early)
-        roots_of(late)
+        inverse_roots(late)
         distances(early)
-        squares_of(late)
-        bends(early)
+        reciprocals(late)
+        squares(early)
         binormals(late)
         energies(early)
         distances(late)
-        bends(late)
+        squares(late)
         moments(early)
         energies(late)
         moments(late)
         for h in range(2):
             for a in range(PACK):
-                nc.scalar.activation(
-                    binu_nx[h][:, a * HALF : (a + 1) * HALF],
-                    binu[a].indirect(nx_sb[:, h * HALF // 16 : (h + 1) * HALF // 16]),
-                    ACT.Copy,
-                )
+                nc.scalar.activation(binu_nx[h][:, a * HALF : (a + 1) * HALF], binu[a].indirect(nx_half[h]), ACT.Copy)
 
         for c0, c1 in OUT_CHUNKS:
-            w = c1 - c0
-            hid = keep.tile([P, w * PACK], BF16, name=f"hid{c0}", align_bytes=64)
-            codes = keep.tile([P, w], U32, name=f"codes{c0}", align_bytes=64)
-            scales = keep.tile([P, w], U8, name=f"scales{c0}", align_bytes=64)
-            res = keep.tile([P, w], F32, name=f"res{c0}")
+            width = c1 - c0
+            hid = keep.tile([P, width * PACK], BF16, name=f"hid{c0}", align_bytes=64)
+            codes = keep.tile([P, width], U32, name=f"codes{c0}", align_bytes=64)
+            code_scales = keep.tile([P, width], U8, name=f"code_scales{c0}", align_bytes=64)
+            res = keep.tile([P, width], F32, name=f"res{c0}")
+            fetched = binu_nx[c0 // HALF][:].rearrange("p (a n) -> p a n", a=PACK)
             nc.vector.tensor_tensor(
                 hid[:].rearrange("p (c i a) -> p c a i", i=4, a=PACK),
                 momu[:, :, c0:c1].rearrange("p a (c i) -> p c a i", i=4),
-                binu_nx[c0 // HALF][:].rearrange("p (a n) -> p a n", a=PACK)[:, :, c0 % HALF : c0 % HALF + w].rearrange(
-                    "p a (c i) -> p c a i", i=4
-                ),
+                fetched[:, :, c0 % HALF : c0 % HALF + width].rearrange("p a (c i) -> p c a i", i=4),
                 ALU.subtract,
             )
-            nc.vector.quantize_mx(out=codes[:].bitcast(FP8X4), scales=scales[:], in_=hid[:])
+            nc.vector.quantize_mx(out=codes[:].bitcast(FP8X4), scales=code_scales[:], in_=hid[:])
             acc = psum.tile([P, S], F32, name="acc")
             nc.tensor.matmul_mx(
-                out=acc[:, 0:w],
+                out=acc[:, 0:width],
                 lhsT=w3w[:].bitcast(FP4X4),
                 lhsT_scale=w3s[:],
                 rhs=codes[:].bitcast(FP8X4),
-                rhs_scale=scales[:],
+                rhs_scale=code_scales[:],
                 start=True,
                 stop=True,
             )
-            nc.scalar.activation(res[:], acc[:, 0:w], ACT.Copy)
+            nc.scalar.activation(res[:], acc[:, 0:width], ACT.Copy)
             nc.sync.dma_start(out=out[:, c0:c1], in_=res[:])

@@ -23,7 +23,6 @@ PASSES = K // (P * PACK)
 QUADS = 4
 HALF = S // 2
 OUT_CHUNKS = [(0, 256), (256, 384), (384, 512)]
-DEALS = [(0, 1), (1, 2), (2, 4)]
 
 
 def tile_picked_ybinor_mom_p_kernel(
@@ -47,8 +46,12 @@ def tile_picked_ybinor_mom_p_kernel(
         stf_sb = keep.tile([P, PACK], F32, name="stf_sb")
         unit_sb = keep.tile([P, PACK], F32, name="unit_sb")
 
-        for plane_tile in (xs, ws_raw[0], ws_raw[1], gs[1]):
-            nc.vector.memset(plane_tile[:].bitcast(I32), 0)
+        win = [keep.tile([P, (4 if a < 2 else 3) * S], F32, name=f"win{a}") for a in range(PACK)]
+        nc.vector.memset(xs[:].bitcast(I32), 0)
+        for plane_tile in (ws_raw[0], ws_raw[1], gs[1]):
+            nc.gpsimd.memset(plane_tile[:].bitcast(I32), 0)
+        for a in range(PACK):
+            (nc.vector if a < 2 else nc.gpsimd).memset(win[a][:, 2 * S :], 0.0)
 
         def load_scales(dst, src, passes):
             for q in range(QUADS):
@@ -60,11 +63,12 @@ def tile_picked_ybinor_mom_p_kernel(
         nc.sync.dma_start(offs_sb[:], offs)
         for o in range(PASSES):
             nc.sync.dma_start(out=xw[o][:], in_=x_words[o].rearrange("p c r -> p (c r)").bitcast(I32))
-        for q in range(QUADS):
-            nc.sync.dma_start(
-                out=xs[32 * q : 32 * q + 4 * PASSES, :].bitcast(I32),
-                in_=x_scales[:, 4 * q : 4 * q + 4, :].bitcast(I32),
-            )
+            if o == 0:
+                for q in range(QUADS):
+                    nc.sync.dma_start(
+                        out=xs[32 * q : 32 * q + 4 * PASSES, :].bitcast(I32),
+                        in_=x_scales[:, 4 * q : 4 * q + 4, :].bitcast(I32),
+                    )
         for w, (words, scales) in enumerate(((w2_words, w2_scales), (w1_words, w1_scales))):
             nc.sync.dma_start(
                 out=ww_raw[w][:].bitcast(I32).rearrange("p (o c) -> p o c", o=PASSES),
@@ -86,33 +90,29 @@ def tile_picked_ybinor_mom_p_kernel(
         nc.vector.tensor_copy(gw[1][:], xw[1][:].bitcast(U32).indirect(offs_sb[:]))
 
         cols = PASSES * P
-        ww_first = [keep.tile([P, 1, 2 * cols], U8, name=f"ww_first{w}", align_bytes=64) for w in range(2)]
-        ws_first = [keep.tile([P, 1, cols], U8, name=f"ws_first{w}", align_bytes=64) for w in range(2)]
         later = PACK - 1
-        dealt = keep.tile([P, 2, 3 * later * cols], U8, name="dealt", tag="xw1", align_bytes=64)
-        ww_later = [dealt[:, w, 0 : 2 * later * cols].rearrange("p (a g) -> p a g", a=later) for w in range(2)]
-        ws_later = [dealt[:, w, 2 * later * cols :].rearrange("p (a g) -> p a g", a=later) for w in range(2)]
-
-        def dealt_words(w, a0, a1):
-            return ww_first[w][:] if a0 == 0 else ww_later[w][:, a0 - 1 : a1 - 1, :]
-
-        def dealt_scales(w, a0, a1):
-            return ws_first[w][:] if a0 == 0 else ws_later[w][:, a0 - 1 : a1 - 1, :]
-
-        for a0, a1 in DEALS:
-            for w in range(2):
-                word_cols = ww_raw[w][:].bitcast(U16).rearrange("p (g a) -> p a g", a=PACK)
-                scale_cols = ws_raw[w][:].rearrange("p (g a) -> p a g", a=PACK)
-                nc.vector.tensor_copy(dealt_words(w, a0, a1).bitcast(U16), word_cols[:, a0:a1, :])
-                nc.vector.tensor_copy(dealt_scales(w, a0, a1), scale_cols[:, a0:a1, :])
+        ww, ws = [], []
+        for w in range(2):
+            word_cols = ww_raw[w][:].bitcast(U16).rearrange("p (g a) -> p g a", a=PACK)
+            scale_cols = ws_raw[w][:].rearrange("p (g a) -> p g a", a=PACK)
+            ww_first = keep.tile([P, 2 * cols], U8, name=f"ww_first{w}", align_bytes=64)
+            ws_first = keep.tile([P, cols], U8, name=f"ws_first{w}", align_bytes=64)
+            ws_later = keep.tile([P, later, cols], U8, name=f"ws_later{w}", align_bytes=64)
+            nc.vector.tensor_copy(ww_first[:].bitcast(U16), word_cols[:, :, 0])
+            nc.vector.tensor_copy(ws_first[:], scale_cols[:, :, 0])
+            nc.vector.tensor_copy(ws_later[:].rearrange("p a g -> p g a"), scale_cols[:, :, 1:PACK])
+            ww_later = keep.tile([P, later, 2 * cols], U8, name=f"ww_later{w}", tag=f"ws_raw{w}", align_bytes=64)
+            nc.vector.tensor_copy(ww_later[:].bitcast(U16).rearrange("p a g -> p g a"), word_cols[:, :, 1:PACK])
+            ww.append([ww_first[:]] + [ww_later[:, a, :] for a in range(later)])
+            ws.append([ws_first[:]] + [ws_later[:, a, :] for a in range(later)])
 
         def product(a, w):
             acc = psum.tile([P, S], F32, name="acc")
             for o in range(PASSES):
                 nc.tensor.matmul_mx(
                     out=acc[:],
-                    lhsT=dealt_words(w, a, a + 1)[:, 0, 2 * o * P : 2 * (o + 1) * P].bitcast(FP4X4),
-                    lhsT_scale=dealt_scales(w, a, a + 1)[:, 0, o * P : (o + 1) * P],
+                    lhsT=ww[w][a][:, 2 * o * P : 2 * (o + 1) * P].bitcast(FP4X4),
+                    lhsT_scale=ws[w][a][:, o * P : (o + 1) * P],
                     rhs=gw[o][:].bitcast(FP8X4),
                     rhs_scale=gs[o][:],
                     start=(o == 0),
@@ -124,9 +124,7 @@ def tile_picked_ybinor_mom_p_kernel(
             return [keep.tile([P, S], F32, name=f"{name}{a}")[:] for a in range(count)]
 
         last = PACK - 1
-        th_et = [keep.tile([P, 2 * S], F32, name=f"th_et{a}") for a in range(PACK)]
-        th = [th_et[a][:, 0:S] for a in range(PACK)]
-        et = [th_et[a][:, S : 2 * S] for a in range(PACK)]
+        th, et = ([win[a][:, j * S : (j + 1) * S] for a in range(PACK)] for j in range(2))
         roots = keep.tile([P, 2 * S], F32, name="roots")
         root = [roots[:, (a % 2) * S : (a % 2 + 1) * S] for a in range(PACK)]
         tw = planes("tw", last) + [roots[:, HALF : HALF + S]]
@@ -145,24 +143,33 @@ def tile_picked_ybinor_mom_p_kernel(
             else:
                 nc.scalar.activation(et[a], et_ps[:], ACT.Copy)
             nc.scalar.activation(th[a], ex_ps[:], ACT.Tanh)
-            for h in range(2):
-                nc.vector.tensor_copy(tn[a][:, h * HALF : (h + 1) * HALF], et[a].indirect(nx_half[h]))
+            if a == last:
+                nc.vector.tensor_copy(tn[a], win[a][:, S : 3 * S].indirect(nx_sb[:]))
+            else:
+                nc.scalar.activation(tn[a], win[a][:, S : 3 * S].indirect(nx_sb[:]), ACT.Copy)
             nc.vector.tensor_tensor(tw[a], tn[a], et[a], ALU.subtract)
             nc.scalar.activation(turn[a], tw[a], ACT.Tanh)
 
-        def fraction(a):
-            nc.scalar.activation(v[a], th_et[a][:].indirect(nx_sb[:]), ACT.Copy, bias=2.5)
-            nc.vector.scalar_tensor_tensor(y1[a], th[a], 0.25, v[a], ALU.mult, ALU.add)
-            nc.vector.scalar_tensor_tensor(y[a], th[a], 2.0, y1[a], ALU.add, ALU.mult)
+        def numerator(a):
             nc.vector.scalar_tensor_tensor(num[a], v[a], -0.5, turn[a], ALU.add, ALU.mult)
 
-        up_to_tanh(0)
-        fraction(0)
-        for a in range(1, PACK):
+        def fraction(a):
+            if a < 2:
+                nc.vector.tensor_scalar(v[a], win[a][:].indirect(nx_sb[:]), 1.0, 2.5, ALU.mult, ALU.add)
+            else:
+                nc.scalar.activation(v[a], win[a][:, 0 : 2 * S].indirect(nx_sb[:]), ACT.Copy, bias=2.5)
+            nc.vector.scalar_tensor_tensor(y1[a], th[a], 0.25, v[a], ALU.mult, ALU.add)
+            nc.vector.scalar_tensor_tensor(y[a], th[a], 2.0, y1[a], ALU.add, ALU.mult)
+            if a < 2:
+                numerator(a)
+
+        for a in range(PACK):
             up_to_tanh(a)
         nc.vector.scalar_tensor_tensor(tw2[last], tw[last], 0.3, tw[last], ALU.mult, ALU.mult)
-        for a in range(1, PACK):
+        for a in range(PACK):
             fraction(a)
+        for a in range(2, PACK):
+            numerator(a)
 
         rest_rows = rest.rearrange("(p a) c -> p a c", a=PACK)
         rest_sb = [keep.tile([P, 2, S], F32, name=f"rest{o}", tag=gw_tags[o], align_bytes=64) for o in range(2)]
@@ -174,7 +181,7 @@ def tile_picked_ybinor_mom_p_kernel(
         nc.gpsimd.memset(w3s[:].bitcast(I32), 0)
         load_scales(w3s, w3_scales, 1)
 
-        safe = keep.tile([P, PACK], F32, name="safe", tag="ws_raw1", align_bytes=64)
+        safe = keep.tile([P, PACK], F32, name="safe", tag="ww_raw1", align_bytes=64)
         uinv = keep.tile([P, PACK], F32, name="uinv")
         nc.vector.scalar_tensor_tensor(safe[:], unit_sb[:], 0.0, unit_sb[:], ALU.is_equal, ALU.add)
         nc.vector.reciprocal(uinv[:], safe[:])
@@ -188,7 +195,10 @@ def tile_picked_ybinor_mom_p_kernel(
 
         def reciprocals(pair):
             for a in pair:
-                nc.scalar.activation(rec[a], root[a], ACT.Square)
+                if a < 2:
+                    nc.vector.tensor_tensor(rec[a], root[a], root[a], ALU.mult)
+                else:
+                    nc.scalar.activation(rec[a], root[a], ACT.Square)
 
         def binormals(pair):
             for a in pair:

@@ -138,7 +138,7 @@ def tile_picked_ybinor_mom_p_kernel(
         def up_to_tanh(a):
             et_ps = product(a, 0)
             ex_ps = product(a, 1)
-            if a == last:
+            if a % 2 == 1:
                 nc.vector.tensor_copy(et[a], et_ps[:])
             else:
                 nc.scalar.activation(et[a], et_ps[:], ACT.Copy)
@@ -195,10 +195,7 @@ def tile_picked_ybinor_mom_p_kernel(
 
         def reciprocals(pair):
             for a in pair:
-                if a < 2:
-                    nc.vector.tensor_tensor(rec[a], root[a], root[a], ALU.mult)
-                else:
-                    nc.scalar.activation(rec[a], root[a], ACT.Square)
+                nc.scalar.activation(rec[a], root[a], ACT.Square)
 
         def binormals(pair):
             for a in pair:

import math
from contextlib import ExitStack

import concourse.mybir as mybir

K, T, S, N, H = 1024, 1024, 512, 128, 512
FLOPS = 2 * S * (2 * K * H + H * N)

F32 = mybir.dt.float32
BF16 = mybir.dt.bfloat16
I32 = mybir.dt.int32
U32 = mybir.dt.uint32
U16 = mybir.dt.uint16
U8 = mybir.dt.uint8
FP8X4 = mybir.dt.float8_e4m3fn_x4
FP4X4 = mybir.dt.float4_e2m1fn_x4
ALU = mybir.AluOpType
ACT = mybir.ActivationFunctionType

P = 128
PACK = 4
PASSES = K // (P * PACK)
QUADS = 4
HALF = S // 2
OUT_CHUNKS = [(0, 256), (256, 384), (384, 512)]


def tile_picked_ybinor_mom_p_kernel(
    tc, x_words, x_scales, w1_words, w1_scales, w2_words, w2_scales, rest, stf, unit, w3_words, w3_scales, offs, nx, out
):
    nc = tc.nc
    with ExitStack() as ctx:
        lists = ctx.enter_context(tc.tile_pool(name="lists", bufs=1))
        keep = ctx.enter_context(tc.tile_pool(name="keep", bufs=1))
        psum = ctx.enter_context(tc.psum_pool(name="psum", bufs=8))

        offs_sb = lists.tile([P, S // 16], U16, name="offs_sb")
        nx_sb = lists.tile([P, S // 16], U16, name="nx_sb")
        nx_half = [nx_sb[:, h * HALF // 16 : (h + 1) * HALF // 16] for h in range(2)]

        xw = [keep.tile([P, T], I32, name=f"xw{o}", align_bytes=64) for o in range(PASSES)]
        xs = keep.tile([P, T], U8, name="xs", align_bytes=64)
        ww_raw = [keep.tile([P, PASSES * 2 * H], U8, name=f"ww_raw{w}", align_bytes=64) for w in range(2)]
        ws_raw = [keep.tile([P, PASSES * H], U8, name=f"ws_raw{w}", align_bytes=64) for w in range(2)]
        gs = [keep.tile([P, S], U8, name=f"gs{o}", align_bytes=64) for o in range(PASSES)]
        stf_sb = keep.tile([P, PACK], F32, name="stf_sb")
        unit_sb = keep.tile([P, PACK], F32, name="unit_sb")

        win = [keep.tile([P, (4 if a < 2 else 3) * S], F32, name=f"win{a}") for a in range(PACK)]
        nc.vector.memset(xs[:].bitcast(I32), 0)
        for plane_tile in (ws_raw[0], ws_raw[1], gs[1]):
            nc.gpsimd.memset(plane_tile[:].bitcast(I32), 0)
        for a in range(PACK):
            (nc.vector if a < 2 else nc.gpsimd).memset(win[a][:, 2 * S :], 0.0)

        def load_scales(dst, src, passes):
            for q in range(QUADS):
                nc.sync.dma_start(
                    out=dst[32 * q : 32 * q + 4, :].bitcast(I32).rearrange("r (o c) -> r o c", o=passes),
                    in_=src[:, 4 * q : 4 * q + 4, :].bitcast(I32).rearrange("o r c -> r o c"),
                )

        nc.sync.dma_start(offs_sb[:], offs)
        for o in range(PASSES):
            nc.sync.dma_start(out=xw[o][:], in_=x_words[o].rearrange("p c r -> p (c r)").bitcast(I32))
            if o == 0:
                for q in range(QUADS):
                    nc.sync.dma_start(
                        out=xs[32 * q : 32 * q + 4 * PASSES, :].bitcast(I32),
                        in_=x_scales[:, 4 * q : 4 * q + 4, :].bitcast(I32),
                    )
        for w, (words, scales) in enumerate(((w2_words, w2_scales), (w1_words, w1_scales))):
            nc.sync.dma_start(
                out=ww_raw[w][:].bitcast(I32).rearrange("p (o c) -> p o c", o=PASSES),
                in_=words.bitcast(I32).rearrange("o p c -> p o c"),
            )
            load_scales(ws_raw[w], scales, PASSES)
        nc.sync.dma_start(nx_sb[:], nx)
        nc.gpsimd.dma_start(out=unit_sb[:], in_=unit.rearrange("(p a) o -> p (a o)", a=PACK))
        nc.gpsimd.dma_start(out=stf_sb[:], in_=stf.rearrange("(p a) o -> p (a o)", a=PACK))

        gw_tags = ("gw0", "xs")
        gw = [keep.tile([P, S], U32, name=f"gw{o}", tag=gw_tags[o], align_bytes=64) for o in range(PASSES)]
        nc.vector.tensor_copy(gw[0][:], xw[0][:].bitcast(U32).indirect(offs_sb[:]))
        nc.vector.tensor_copy(gs[0][:], xs[:].indirect(offs_sb[:]))
        for q in range(QUADS):
            nc.scalar.dma_start(
                out=gs[1][32 * q : 32 * q + 4, :].bitcast(I32), in_=gs[0][32 * q + 4 : 32 * q + 8, :].bitcast(I32)
            )
        nc.vector.tensor_copy(gw[1][:], xw[1][:].bitcast(U32).indirect(offs_sb[:]))

        cols = PASSES * P
        later = PACK - 1
        ww, ws = [], []
        for w in range(2):
            word_cols = ww_raw[w][:].bitcast(U16).rearrange("p (g a) -> p g a", a=PACK)
            scale_cols = ws_raw[w][:].rearrange("p (g a) -> p g a", a=PACK)
            ww_first = keep.tile([P, 2 * cols], U8, name=f"ww_first{w}", align_bytes=64)
            ws_first = keep.tile([P, cols], U8, name=f"ws_first{w}", align_bytes=64)
            ws_later = keep.tile([P, later, cols], U8, name=f"ws_later{w}", align_bytes=64)
            nc.vector.tensor_copy(ww_first[:].bitcast(U16), word_cols[:, :, 0])
            nc.vector.tensor_copy(ws_first[:], scale_cols[:, :, 0])
            nc.vector.tensor_copy(ws_later[:].rearrange("p a g -> p g a"), scale_cols[:, :, 1:PACK])
            ww_later = keep.tile([P, later, 2 * cols], U8, name=f"ww_later{w}", tag=f"ws_raw{w}", align_bytes=64)
            nc.vector.tensor_copy(ww_later[:].bitcast(U16).rearrange("p a g -> p g a"), word_cols[:, :, 1:PACK])
            ww.append([ww_first[:]] + [ww_later[:, a, :] for a in range(later)])
            ws.append([ws_first[:]] + [ws_later[:, a, :] for a in range(later)])

        def product(a, w):
            acc = psum.tile([P, S], F32, name="acc")
            for o in range(PASSES):
                nc.tensor.matmul_mx(
                    out=acc[:],
                    lhsT=ww[w][a][:, 2 * o * P : 2 * (o + 1) * P].bitcast(FP4X4),
                    lhsT_scale=ws[w][a][:, o * P : (o + 1) * P],
                    rhs=gw[o][:].bitcast(FP8X4),
                    rhs_scale=gs[o][:],
                    start=(o == 0),
                    stop=(o == PASSES - 1),
                )
            return acc

        def planes(name, count=PACK):
            return [keep.tile([P, S], F32, name=f"{name}{a}")[:] for a in range(count)]

        last = PACK - 1
        th, et = ([win[a][:, j * S : (j + 1) * S] for a in range(PACK)] for j in range(2))
        roots = keep.tile([P, 2 * S], F32, name="roots")
        root = [roots[:, (a % 2) * S : (a % 2 + 1) * S] for a in range(PACK)]
        tw = planes("tw", last) + [roots[:, HALF : HALF + S]]
        binu_nx = [keep.tile([P, PACK * HALF], F32, name=f"binu_nx{h}") for h in range(2)]
        dist = [binu_nx[a // 2][:, (a % 2) * S : (a % 2 + 1) * S] for a in range(PACK)]
        tn, turn, tw2, v, y1, y, num, rec, binu, bend, ener = (
            planes(nm) for nm in ("tn", "turn", "tw2", "v", "y1", "y", "num", "rec", "binu", "bend", "ener")
        )
        momu = keep.tile([P, PACK, S], F32, name="momu")

        def up_to_tanh(a):
            et_ps = product(a, 0)
            ex_ps = product(a, 1)
            if a % 2 == 1:
                nc.vector.tensor_copy(et[a], et_ps[:])
            else:
                nc.scalar.activation(et[a], et_ps[:], ACT.Copy)
            nc.scalar.activation(th[a], ex_ps[:], ACT.Tanh)
            if a == last:
                nc.vector.tensor_copy(tn[a], win[a][:, S : 3 * S].indirect(nx_sb[:]))
            else:
                nc.scalar.activation(tn[a], win[a][:, S : 3 * S].indirect(nx_sb[:]), ACT.Copy)
            nc.vector.tensor_tensor(tw[a], tn[a], et[a], ALU.subtract)
            nc.scalar.activation(turn[a], tw[a], ACT.Tanh)

        def numerator(a):
            nc.vector.scalar_tensor_tensor(num[a], v[a], -0.5, turn[a], ALU.add, ALU.mult)

        def fraction(a):
            if a < 2:
                nc.vector.tensor_scalar(v[a], win[a][:].indirect(nx_sb[:]), 1.0, 2.5, ALU.mult, ALU.add)
            else:
                nc.scalar.activation(v[a], win[a][:, 0 : 2 * S].indirect(nx_sb[:]), ACT.Copy, bias=2.5)
            nc.vector.scalar_tensor_tensor(y1[a], th[a], 0.25, v[a], ALU.mult, ALU.add)
            nc.vector.scalar_tensor_tensor(y[a], th[a], 2.0, y1[a], ALU.add, ALU.mult)
            if a < 2:
                numerator(a)

        for a in range(PACK):
            up_to_tanh(a)
        nc.vector.scalar_tensor_tensor(tw2[last], tw[last], 0.3, tw[last], ALU.mult, ALU.mult)
        for a in range(PACK):
            fraction(a)
        for a in range(2, PACK):
            numerator(a)

        rest_rows = rest.rearrange("(p a) c -> p a c", a=PACK)
        rest_sb = [keep.tile([P, 2, S], F32, name=f"rest{o}", tag=gw_tags[o], align_bytes=64) for o in range(2)]
        for o in range(2):
            nc.sync.dma_start(out=rest_sb[o][:], in_=rest_rows[:, 2 * o : 2 * o + 2, :])
        w3w = keep.tile([P, 2 * N], U8, name="w3w", tag="gs0", align_bytes=64)
        nc.sync.dma_start(out=w3w[:].bitcast(I32), in_=w3_words[0].bitcast(I32))
        w3s = keep.tile([P, N], U8, name="w3s", tag="gs1", align_bytes=64)
        nc.gpsimd.memset(w3s[:].bitcast(I32), 0)
        load_scales(w3s, w3_scales, 1)

        safe = keep.tile([P, PACK], F32, name="safe", tag="ww_raw1", align_bytes=64)
        uinv = keep.tile([P, PACK], F32, name="uinv")
        nc.vector.scalar_tensor_tensor(safe[:], unit_sb[:], 0.0, unit_sb[:], ALU.is_equal, ALU.add)
        nc.vector.reciprocal(uinv[:], safe[:])

        def col(t, a):
            return t[:, a : a + 1]

        def inverse_roots(pair):
            for a in pair:
                nc.scalar.activation(root[a], y[a], ACT.Abs_reciprocal_sqrt, bias=0.3, scale=0.25)

        def reciprocals(pair):
            for a in pair:
                nc.scalar.activation(rec[a], root[a], ACT.Square)

        def binormals(pair):
            for a in pair:
                nc.vector.scalar_tensor_tensor(binu[a], num[a], col(unit_sb, a), rec[a], ALU.mult, ALU.mult)

        def distances(pair):
            for a in pair:
                nc.vector.scalar_tensor_tensor(
                    dist[a], binu[a], col(uinv, a), rest_sb[a // 2][:, a % 2, :], ALU.mult, ALU.subtract
                )

        def squares(pair):
            for a in pair:
                nc.scalar.activation(bend[a], dist[a], ACT.Square)
            for a in pair:
                if a != last:
                    nc.scalar.activation(tw2[a], tw[a], ACT.Square, scale=math.sqrt(0.3))

        def energies(pair):
            for a in pair:
                nc.vector.scalar_tensor_tensor(ener[a], bend[a], col(stf_sb, a), tw2[a], ALU.mult, ALU.add)

        def moments(pair):
            for a in pair:
                nc.vector.tensor_tensor(momu[:, a, :], binu[a], ener[a], ALU.mult)

        early, late = (0, 1), (2, 3)
        inverse_roots(early)
        reciprocals(early)
        binormals(early)
        inverse_roots(late)
        distances(early)
        reciprocals(late)
        squares(early)
        binormals(late)
        energies(early)
        distances(late)
        squares(late)
        moments(early)
        energies(late)
        moments(late)
        for h in range(2):
            for a in range(PACK):
                nc.scalar.activation(binu_nx[h][:, a * HALF : (a + 1) * HALF], binu[a].indirect(nx_half[h]), ACT.Copy)

        for c0, c1 in OUT_CHUNKS:
            width = c1 - c0
            hid = keep.tile([P, width * PACK], BF16, name=f"hid{c0}", align_bytes=64)
            codes = keep.tile([P, width], U32, name=f"codes{c0}", align_bytes=64)
            code_scales = keep.tile([P, width], U8, name=f"code_scales{c0}", align_bytes=64)
            res = keep.tile([P, width], F32, name=f"res{c0}")
            fetched = binu_nx[c0 // HALF][:].rearrange("p (a n) -> p a n", a=PACK)
            nc.vector.tensor_tensor(
                hid[:].rearrange("p (c i a) -> p c a i", i=4, a=PACK),
                momu[:, :, c0:c1].rearrange("p a (c i) -> p c a i", i=4),
                fetched[:, :, c0 % HALF : c0 % HALF + width].rearrange("p a (c i) -> p c a i", i=4),
                ALU.subtract,
            )
            nc.vector.quantize_mx(out=codes[:].bitcast(FP8X4), scales=code_scales[:], in_=hid[:])
            acc = psum.tile([P, S], F32, name="acc")
            nc.tensor.matmul_mx(
                out=acc[:, 0:width],
                lhsT=w3w[:].bitcast(FP4X4),
                lhsT_scale=w3s[:],
                rhs=codes[:].bitcast(FP8X4),
                rhs_scale=code_scales[:],
                start=True,
                stop=True,
            )
            nc.scalar.activation(res[:], acc[:, 0:width], ACT.Copy)
            nc.sync.dma_start(out=out[:, c0:c1], in_=res[:])
